import numpy as np, ml_dtypes
CORES = [17,81,89,18,82,90]
N = 6
T = 64
def entries(a): return a.T.reshape(-1)
def pack(v, P): return np.ascontiguousarray(np.asarray(v, np.int32).reshape(-1, P).T)
def lists(rng, how):
    n = rng.integers(0, T + 1, N)
    if how == "none": n[rng.integers(N)] = 0; n[0] = 0
    if how == "full": n[:] = T
    if how == "one": n[:] = 1
    if how == "lone": z = int(rng.integers(N)); n[:] = 0; n[z] = int(rng.integers(1, T + 1))
    if how == "void": n[:] = 0
    return {"ln": np.broadcast_to(pack(np.concatenate([n, np.zeros(32 - N, np.int64)]), 16), (N, 16, 2)).copy()}
def setup_inputs(rng):
    return dict({"x": rng.standard_normal((N, 128, T), dtype=np.float32).astype(ml_dtypes.bfloat16)}, **lists(rng, "uniform"))
def setup_inputs_full(rng):
    d = setup_inputs(rng); d.update(lists(rng, "full"))
    for k in ("x",): d[k] = (d[k].astype(np.float32) * 1048576.0).astype(d[k].dtype)
    return d
def setup_inputs_lone(rng):
    d = setup_inputs(rng); d.update(lists(rng, "lone"))
    for k in ("x",): d[k] = (d[k].astype(np.float32) * (1 / 1024.0)).astype(d[k].dtype)
    return d
def setup_inputs_none(rng):
    d = setup_inputs(rng); d.update(lists(rng, "none"))
    return d
def setup_inputs_one(rng):
    d = setup_inputs(rng); d.update(lists(rng, "one"))
    return d
def setup_inputs_void(rng):
    d = setup_inputs(rng); d.update(lists(rng, "void"))
    return d
def check_inputs(x):
    bad = []
    if x["ln"].min() < 0 or x["ln"].max() >= T + 1: bad.append("ln out of range")
    if entries(x["ln"][0])[N:].any(): bad.append("an entry from N on isn't 0")
    if not all(np.array_equal(a, x["ln"][0]) for a in x["ln"]): bad.append("ln isn't alike on all ranks")
    return bad
def reference(x, ln):
    n = entries(ln[0]); got = np.concatenate([x[r][:, :n[r]] for r in range(N)], axis=1)
    y = np.zeros((128, N * T), x.dtype); y[:, :got.shape[1]] = got
    return {"y": np.broadcast_to(y, (N, 128, N * T))}

@@ -1,0 +1,154 @@
+from concourse.bass import DstId, RemoteDMATransfer
+from concourse.mybir import AluOpType
+
+N = 6
+TC = 64
+NO = N * TC
+KC = NO // 16
+FAR = 1024
+
+SCRATCH = {
+    "win": ("sbuf", [128, NO + 8], "bfloat16"),
+    "yb": ("sbuf", [128, NO], "bfloat16"),
+    "lnb": ("sbuf", [16, 2], "int32"),
+    "lnf": ("sbuf", [16, 1], "float32"),
+    "vi": ("sbuf", [128, KC], "int32"),
+    "va": ("sbuf", [128, KC], "int32"),
+    "vb": ("sbuf", [128, KC], "int32"),
+    "ki": ("sbuf", [16, N], "float32"),
+    "tri": ("sbuf", [16, 2 * N], "bfloat16"),
+    "rr": ("sbuf", [16, 2 * N], "bfloat16"),
+    "ones": ("sbuf", [16, 128], "bfloat16"),
+    "cst": ("sbuf", [16, 2 * N], "bfloat16"),
+    "ps": ("psum", [128, 2 * N], "float32"),
+    "pp": ("sbuf", [128, 8 * KC], "float32"),
+    "q1": ("sbuf", [128, 4 * KC], "float32"),
+    "q2": ("sbuf", [128, 2 * KC], "float32"),
+    "q3": ("sbuf", [128, KC], "float32"),
+    "off": ("sbuf", [128, KC], "uint16"),
+}
+SEMAPHORES = ["ldx", "ldl", "gi", "vc", "vj", "vl", "vr", "mm", "vm", "vt", "p1", "p2", "snt", "gat", "st"]
+
+
+def _bits(m):
+    return bin(m).count("1")
+
+
+def _plan(cores, topo):
+    chips = []
+    for c in cores:
+        if topo.chip(c) not in chips:
+            chips.append(topo.chip(c))
+    members = {ch: [c for c in cores if topo.chip(c) == ch] for ch in chips}
+    slot, first, k = {}, {}, 0
+    for ch in chips:
+        first[ch] = k
+        for c in members[ch]:
+            slot[c] = k
+            k += 1
+    carry = {c: [] for c in cores}
+    for ch in chips:
+        todo = [o for o in chips if o != ch]
+        able = {o: [c for c in members[ch] if all(topo.may_write(c, d) for d in members[o])] for o in todo}
+        todo.sort(key=lambda o: len(able[o]))
+        for o in todo:
+            carry[min(able[o], key=lambda c: len(carry[c]))].append(o)
+    return chips, members, slot, first, carry
+
+
+def _mask(core, cores, topo):
+    m = -1
+    for d in cores:
+        if d != core:
+            m &= topo.mask(core, d)
+    return m
+
+
+def rank_program(g, core, T, topo):
+    if T.rank_of(core) is None:
+        return
+    S = T.sem
+    A = AluOpType
+    cores = list(T.cores)
+    chips, members, slot, first, carry = _plan(cores, topo)
+    me = topo.chip(core)
+    mask = _mask(core, cores, topo)
+    own = T.win[:, slot[core] * TC:(slot[core] + 1) * TC]
+    piece = T.win[:, first[me] * TC:(first[me] + len(members[me])) * TC]
+
+    g.sync.dma_start(own, T.x[:]).then_inc(S.ldx, 16)
+    g.scalar.dma_start(T.lnb[:], T.ln[:]).then_inc(S.ldl, 16)
+
+    g.iota(T.vi[:], [[128, KC]], 0, 1).then_inc(S.gi, 1)
+    g.iota(T.ki[:], [[1, N]], 0, -1, allow_small_or_imprecise_dtypes=True).then_inc(S.gi, 1)
+    g.wait_ge(S.ldx, 16)
+    sent = 0
+    for d in members[me]:
+        if d != core:
+            rid, pid, _ = topo.addr(d)
+            g.remote_dma(own, own, S.p1, S.snt, pid, rid, mask)
+            sent += _bits(mask)
+    n1 = sum(_bits(_mask(d, cores, topo)) for d in members[me] if d != core)
+    n2 = sum(_bits(_mask(s, cores, topo)) for s in cores if me in carry[s])
+    if carry[core]:
+        g.wait_ge(S.p1, n1)
+        dsts = [d for o in carry[core] for d in members[o]]
+        g.remote_dma_fused(
+            [RemoteDMATransfer(dst_ids=[DstId(rid=topo.addr(d)[0], pnc=topo.addr(d)[1]) for d in dsts],
+                               dma_engine_mask=mask, remote_sem=S.p2, srcs=[piece], dsts=[piece for d in dsts])],
+            local_sem=S.snt)
+        sent += _bits(mask)
+    g.wait_ge(S.snt, sent)
+
+    v = g.vector
+    nc = 0
+    v.memset(T.win[:, NO:NO + 8], 0.0).then_inc(S.vc, 1)
+    v.memset(T.ones[:], 1.0).then_inc(S.vc, 1)
+    v.memset(T.cst[0:1, 0:N], 0.0).then_inc(S.vc, 1)
+    v.memset(T.pp[:, 7 * KC:8 * KC], 0.0).then_inc(S.vc, 1)
+    nc += 4
+    for i in range(N):
+        d = (slot[cores[i + 1]] - slot[cores[i]]) * TC if i + 1 < N else FAR
+        v.memset(T.cst[0:1, N + i:N + i + 1], float(d)).then_inc(S.vc, 1)
+        nc += 1
+    v.wait_ge(S.gi, 2)
+    v.tensor_scalar(T.va[:], T.vi[:], 15, None, A.bitwise_and).then_inc(S.vj, 1)
+    v.tensor_scalar(T.vb[:], T.vi[:], 3, 0xFFF0, A.logical_shift_right, A.bitwise_and).then_inc(S.vj, 1)
+    v.tensor_scalar(T.tri[:, 0:N], T.ki[:], 0.0, None, A.is_ge).then_inc(S.vc, 1)
+    v.tensor_scalar(T.tri[:, N:2 * N], T.ki[:], 0.0, -1.0, A.is_equal, A.mult).then_inc(S.vc, 1)
+    v.wait_ge(S.vj, 2)
+    jj = T.pp[:, 6 * KC:7 * KC]
+    v.tensor_tensor(jj, T.va[:], T.vb[:], A.add).then_inc(S.vc, 1)
+    nc += 3
+
+    v.wait_ge(S.ldl, 16)
+    v.tensor_copy(T.lnf[:], T.lnb[:, 0:1]).then_inc(S.vl, 1)
+    v.wait_ge(S.vl, 1)
+    v.wait_ge(S.vc, nc)
+    v.tensor_scalar(T.rr[:], T.tri[:], T.lnf[:, 0:1], None, A.mult).then_inc(S.vr, 1)
+    t = g.tensor
+    t.wait_ge(S.vc, nc)
+    t.matmul(T.ps[:], T.ones[0:1, :], T.cst[0:1, :], True, False)
+    t.wait_ge(S.vr, 1)
+    t.matmul(T.ps[:], T.ones[:], T.rr[:], False, True).then_inc(S.mm, 1)
+    v.wait_ge(S.mm, 1)
+    for s in range(N):
+        v.tensor_scalar(T.pp[:, s * KC:(s + 1) * KC], jj, T.ps[:, s:s + 1], T.ps[:, N + s:N + s + 1],
+                        A.is_ge, A.mult).then_inc(S.vm, 1)
+    v.wait_ge(S.vm, N)
+    v.tensor_tensor(T.q1[:], T.pp[:, 0:4 * KC], T.pp[:, 4 * KC:8 * KC], A.add).then_inc(S.vt, 1)
+    v.wait_ge(S.vt, 1)
+    v.tensor_tensor(T.q2[:], T.q1[:, 0:2 * KC], T.q1[:, 2 * KC:4 * KC], A.add).then_inc(S.vt, 1)
+    v.wait_ge(S.vt, 2)
+    v.tensor_tensor(T.q3[:], T.q2[:, 0:KC], T.q2[:, KC:2 * KC], A.add).then_inc(S.vt, 1)
+    v.wait_ge(S.vt, 3)
+    v.tensor_scalar(T.off[:], T.q3[:], float(NO), None, A.min).then_inc(S.vt, 1)
+    v.wait_ge(S.vt, 4)
+
+    v.wait_ge(S.ldx, 16)
+    v.wait_ge(S.p1, n1)
+    v.wait_ge(S.p2, n2)
+    v.tensor_copy(T.yb[:], T.win[:, 0:NO + 8].indirect(T.off[:, 0:KC])).then_inc(S.gat, 1)
+    g.sync.wait_ge(S.gat, 1)
+    g.sync.dma_start(T.y[:], T.yb[:]).then_inc(S.st, 16)
+    g.sync.wait_ge(S.st, 16)

@@ -1,15 +1,18 @@
 from concourse.bass import DstId, RemoteDMATransfer
-from concourse.mybir import AluOpType
+from concourse.mybir import AluOpType, ActivationFunctionType
 
 N = 6
 TC = 64
 NO = N * TC
 KC = NO // 16
+LANE = 4
 FAR = 1024
 
 SCRATCH = {
     "win": ("sbuf", [128, NO + 8], "bfloat16"),
     "yb": ("sbuf", [128, NO], "bfloat16"),
+    "xd": ("dram", [128, TC], "bfloat16"),
+    "xr": ("dram", [N, 128, TC], "bfloat16"),
     "lnb": ("sbuf", [16, 2], "int32"),
     "lnf": ("sbuf", [16, 1], "float32"),
     "vi": ("sbuf", [128, KC], "int32"),
@@ -27,7 +30,8 @@ SCRATCH = {
     "q3": ("sbuf", [128, KC], "float32"),
     "off": ("sbuf", [128, KC], "uint16"),
 }
-SEMAPHORES = ["ldx", "ldl", "gi", "vc", "vj", "vl", "vr", "mm", "vm", "vt", "p1", "p2", "snt", "gat", "st"]
+SEMAPHORES = ["ldx", "ldl", "gi", "vc", "vj", "vl", "vr", "mm", "vm", "vt", "ldd", "lda", "pa", "pd", "p1", "p2",
+              "snt", "gat", "st"]
 
 
 def _bits(m):
@@ -53,7 +57,20 @@ def _plan(cores, topo):
         todo.sort(key=lambda o: len(able[o]))
         for o in todo:
             carry[min(able[o], key=lambda c: len(carry[c]))].append(o)
-    return chips, members, slot, first, carry
+    feed = {c: [d for d in members[topo.chip(c)] if d != c] for c in cores}
+    ahead, relay, lane = [], [], {}
+    for s in cores:
+        ch = topo.chip(s)
+        far = [d for o in carry[s] for d in members[o]]
+        if len(carry[s]) > 1:
+            ahead.append((s, slot[s], far))
+            for f in members[ch]:
+                if f != s:
+                    lane[f] = s
+                    relay.append((s, slot[f], slot[f] + 1, far, True))
+        elif far:
+            relay.append((s, first[ch], first[ch] + len(members[ch]), far, False))
+    return slot, feed, ahead, relay, lane
 
 
 def _mask(core, cores, topo):
@@ -64,41 +81,78 @@ def _mask(core, cores, topo):
     return m
 
 
+def _few(m, n):
+    return sum([1 << b for b in range(m.bit_length()) if (m >> b) & 1][:n])
+
+
 def rank_program(g, core, T, topo):
     if T.rank_of(core) is None:
         return
     S = T.sem
     A = AluOpType
     cores = list(T.cores)
-    chips, members, slot, first, carry = _plan(cores, topo)
-    me = topo.chip(core)
-    mask = _mask(core, cores, topo)
-    own = T.win[:, slot[core] * TC:(slot[core] + 1) * TC]
-    piece = T.win[:, first[me] * TC:(first[me] + len(members[me])) * TC]
+    slot, feed, ahead, relay, lane = _plan(cores, topo)
 
+    def engines(c):
+        m = _mask(c, cores, topo)
+        return _few(m, LANE) if c in lane else m
+
+    mask = engines(core)
+    pre = [w for w in ahead if w[0] == core]
+    got = [w for w in ahead if core in w[2]]
+    mine = [w for w in relay if w[0] == core]
+    na = sum(_bits(engines(w[0])) for w in got)
+    nd = sum(_bits(engines(f)) for f in lane if lane[f] == core)
+    n1 = sum(_bits(engines(c)) for c in cores if core in feed[c])
+    n2 = sum(_bits(engines(w[0])) for w in relay if core in w[3])
+    sent = [0]
+
+    def send(src, dst, dsts, sem):
+        g.remote_dma_fused(
+            [RemoteDMATransfer(dst_ids=[DstId(rid=topo.addr(d)[0], pnc=topo.addr(d)[1]) for d in dsts],
+                               dma_engine_mask=mask, remote_sem=sem, srcs=[src], dsts=[dst for d in dsts])],
+            local_sem=S.snt)
+        sent[0] += _bits(mask)
+
+    def slots(lo, hi):
+        return T.win[:, lo * TC:hi * TC]
+
+    k = slot[core]
+    own = slots(k, k + 1)
+    long_rows = core in lane or len(pre) > 0
+
+    if long_rows:
+        g.sync.dma_start(T.xd[:], T.x[:]).then_inc(S.ldd, 16)
     g.sync.dma_start(own, T.x[:]).then_inc(S.ldx, 16)
     g.scalar.dma_start(T.lnb[:], T.ln[:]).then_inc(S.ldl, 16)
+    if got:
+        g.scalar.wait_ge(S.pa, na)
+        for w in got:
+            g.scalar.dma_start(slots(w[1], w[1] + 1), T.xr[w[1]]).then_inc(S.lda, 16)
 
     g.iota(T.vi[:], [[128, KC]], 0, 1).then_inc(S.gi, 1)
     g.iota(T.ki[:], [[1, N]], 0, -1, allow_small_or_imprecise_dtypes=True).then_inc(S.gi, 1)
-    g.wait_ge(S.ldx, 16)
-    sent = 0
-    for d in members[me]:
-        if d != core:
-            rid, pid, _ = topo.addr(d)
-            g.remote_dma(own, own, S.p1, S.snt, pid, rid, mask)
-            sent += _bits(mask)
-    n1 = sum(_bits(_mask(d, cores, topo)) for d in members[me] if d != core)
-    n2 = sum(_bits(_mask(s, cores, topo)) for s in cores if me in carry[s])
-    if carry[core]:
-        g.wait_ge(S.p1, n1)
-        dsts = [d for o in carry[core] for d in members[o]]
-        g.remote_dma_fused(
-            [RemoteDMATransfer(dst_ids=[DstId(rid=topo.addr(d)[0], pnc=topo.addr(d)[1]) for d in dsts],
-                               dma_engine_mask=mask, remote_sem=S.p2, srcs=[piece], dsts=[piece for d in dsts])],
-            local_sem=S.snt)
-        sent += _bits(mask)
-    g.wait_ge(S.snt, sent)
+    if long_rows:
+        g.wait_ge(S.ldd, 16)
+        if core in lane:
+            send(T.xd[:], T.xr[k], [lane[core]], S.pd)
+        for w in pre:
+            send(T.xd[:], T.xr[k], w[2], S.pa)
+        send(T.xd[:], own, feed[core], S.p1)
+    else:
+        g.wait_ge(S.ldx, 16)
+        send(own, own, feed[core], S.p1)
+    if nd:
+        g.wait_ge(S.pd, nd)
+    for w in mine:
+        if w[4]:
+            send(T.xr[w[1]], slots(w[1], w[2]), w[3], S.p2)
+    for w in mine:
+        if not w[4]:
+            g.wait_ge(S.ldx, 16)
+            g.wait_ge(S.p1, n1)
+            send(slots(w[1], w[2]), slots(w[1], w[2]), w[3], S.p2)
+    g.wait_ge(S.snt, sent[0])
 
     v = g.vector
     nc = 0
@@ -143,12 +197,20 @@ def rank_program(g, core, T, topo):
     v.tensor_tensor(T.q3[:], T.q2[:, 0:KC], T.q2[:, KC:2 * KC], A.add).then_inc(S.vt, 1)
     v.wait_ge(S.vt, 3)
     v.tensor_scalar(T.off[:], T.q3[:], float(NO), None, A.min).then_inc(S.vt, 1)
-    v.wait_ge(S.vt, 4)
 
-    v.wait_ge(S.ldx, 16)
-    v.wait_ge(S.p1, n1)
-    v.wait_ge(S.p2, n2)
-    v.tensor_copy(T.yb[:], T.win[:, 0:NO + 8].indirect(T.off[:, 0:KC])).then_inc(S.gat, 1)
-    g.sync.wait_ge(S.gat, 1)
+    window = T.win[:, 0:NO + 8]
+    hk = KC // 2
+    for q in (v, g.scalar):
+        q.wait_ge(S.vt, 4)
+        q.wait_ge(S.vc, nc)
+        q.wait_ge(S.ldx, 16)
+        if got:
+            q.wait_ge(S.lda, 16 * len(got))
+        q.wait_ge(S.p1, n1)
+        q.wait_ge(S.p2, n2)
+    v.tensor_copy(T.yb[:, 0:16 * hk], window.indirect(T.off[:, 0:hk])).then_inc(S.gat, 1)
+    g.scalar.activation(T.yb[:, 16 * hk:NO], window.indirect(T.off[:, hk:KC]),
+                        ActivationFunctionType.Identity, bias=-0.0, scale=1.0).then_inc(S.gat, 1)
+    g.sync.wait_ge(S.gat, 2)
     g.sync.dma_start(T.y[:], T.yb[:]).then_inc(S.st, 16)
     g.sync.wait_ge(S.st, 16)

@@ -5,11 +5,11 @@ N = 6
 TC = 64
 NO = N * TC
 KC = NO // 16
-LANE = 4
 FAR = 1024
 
 SCRATCH = {
     "win": ("sbuf", [128, NO + 8], "bfloat16"),
+    "zz": ("sbuf", [128, 8], "bfloat16"),
     "yb": ("sbuf", [128, NO], "bfloat16"),
     "xd": ("dram", [128, TC], "bfloat16"),
     "xr": ("dram", [N, 128, TC], "bfloat16"),
@@ -18,6 +18,7 @@ SCRATCH = {
     "vi": ("sbuf", [128, KC], "int32"),
     "va": ("sbuf", [128, KC], "int32"),
     "vb": ("sbuf", [128, KC], "int32"),
+    "vq": ("sbuf", [16, N], "int32"),
     "ki": ("sbuf", [16, N], "float32"),
     "tri": ("sbuf", [16, 2 * N], "bfloat16"),
     "rr": ("sbuf", [16, 2 * N], "bfloat16"),
@@ -30,8 +31,8 @@ SCRATCH = {
     "q3": ("sbuf", [128, KC], "float32"),
     "off": ("sbuf", [128, KC], "uint16"),
 }
-SEMAPHORES = ["ldx", "ldl", "gi", "vc", "vj", "vl", "vr", "mm", "vm", "vt", "ldd", "lda", "pa", "pd", "p1", "p2",
-              "snt", "gat", "st"]
+SEMAPHORES = ["ldx", "ldl", "gi", "vc", "vj", "vk", "vl", "vr", "mm", "vm", "vt", "ldd", "lda", "pa", "pd", "p1",
+              "p2", "snt", "gat", "st", "vz", "pz"]
 
 
 def _bits(m):
@@ -81,10 +82,6 @@ def _mask(core, cores, topo):
     return m
 
 
-def _few(m, n):
-    return sum([1 << b for b in range(m.bit_length()) if (m >> b) & 1][:n])
-
-
 def rank_program(g, core, T, topo):
     if T.rank_of(core) is None:
         return
@@ -94,8 +91,7 @@ def rank_program(g, core, T, topo):
     slot, feed, ahead, relay, lane = _plan(cores, topo)
 
     def engines(c):
-        m = _mask(c, cores, topo)
-        return _few(m, LANE) if c in lane else m
+        return _mask(c, cores, topo)
 
     mask = engines(core)
     pre = [w for w in ahead if w[0] == core]
@@ -120,6 +116,7 @@ def rank_program(g, core, T, topo):
     k = slot[core]
     own = slots(k, k + 1)
     long_rows = core in lane or len(pre) > 0
+    v = g.vector
 
     if long_rows:
         g.sync.dma_start(T.xd[:], T.x[:]).then_inc(S.ldd, 16)
@@ -130,8 +127,10 @@ def rank_program(g, core, T, topo):
         for w in got:
             g.scalar.dma_start(slots(w[1], w[1] + 1), T.xr[w[1]]).then_inc(S.lda, 16)
 
+    v.memset(T.zz[:], 0.0).then_inc(S.vz, 1)
     g.iota(T.vi[:], [[128, KC]], 0, 1).then_inc(S.gi, 1)
-    g.iota(T.ki[:], [[1, N]], 0, -1, allow_small_or_imprecise_dtypes=True).then_inc(S.gi, 1)
+    g.wait_ge(S.vz, 1)
+    send(T.zz[:], T.win[:, NO:NO + 8], feed[core], S.pz)
     if long_rows:
         g.wait_ge(S.ldd, 16)
         if core in lane:
@@ -154,25 +153,26 @@ def rank_program(g, core, T, topo):
             send(slots(w[1], w[2]), slots(w[1], w[2]), w[3], S.p2)
     g.wait_ge(S.snt, sent[0])
 
-    v = g.vector
     nc = 0
-    v.memset(T.win[:, NO:NO + 8], 0.0).then_inc(S.vc, 1)
     v.memset(T.ones[:], 1.0).then_inc(S.vc, 1)
     v.memset(T.cst[0:1, 0:N], 0.0).then_inc(S.vc, 1)
     v.memset(T.pp[:, 7 * KC:8 * KC], 0.0).then_inc(S.vc, 1)
-    nc += 4
+    nc += 3
     for i in range(N):
         d = (slot[cores[i + 1]] - slot[cores[i]]) * TC if i + 1 < N else FAR
         v.memset(T.cst[0:1, N + i:N + i + 1], float(d)).then_inc(S.vc, 1)
         nc += 1
-    v.wait_ge(S.gi, 2)
+    v.wait_ge(S.gi, 1)
     v.tensor_scalar(T.va[:], T.vi[:], 15, None, A.bitwise_and).then_inc(S.vj, 1)
+    v.tensor_scalar(T.vq[:], T.vi[0:16, 0:N], 7, None, A.logical_shift_right).then_inc(S.vj, 1)
     v.tensor_scalar(T.vb[:], T.vi[:], 3, 0xFFF0, A.logical_shift_right, A.bitwise_and).then_inc(S.vj, 1)
-    v.tensor_scalar(T.tri[:, 0:N], T.ki[:], 0.0, None, A.is_ge).then_inc(S.vc, 1)
-    v.tensor_scalar(T.tri[:, N:2 * N], T.ki[:], 0.0, -1.0, A.is_equal, A.mult).then_inc(S.vc, 1)
-    v.wait_ge(S.vj, 2)
+    v.wait_ge(S.vj, 3)
+    v.tensor_tensor(T.ki[:], T.vq[:], T.va[0:16, 0:N], A.subtract).then_inc(S.vk, 1)
     jj = T.pp[:, 6 * KC:7 * KC]
     v.tensor_tensor(jj, T.va[:], T.vb[:], A.add).then_inc(S.vc, 1)
+    v.wait_ge(S.vk, 1)
+    v.tensor_scalar(T.tri[:, 0:N], T.ki[:], 0.0, None, A.is_ge).then_inc(S.vc, 1)
+    v.tensor_scalar(T.tri[:, N:2 * N], T.ki[:], 0.0, -1.0, A.is_equal, A.mult).then_inc(S.vc, 1)
     nc += 3
 
     v.wait_ge(S.ldl, 16)
@@ -202,7 +202,7 @@ def rank_program(g, core, T, topo):
     hk = KC // 2
     for q in (v, g.scalar):
         q.wait_ge(S.vt, 4)
-        q.wait_ge(S.vc, nc)
+        q.wait_ge(S.pz, n1)
         q.wait_ge(S.ldx, 16)
         if got:
             q.wait_ge(S.lda, 16 * len(got))

@@ -5,10 +5,15 @@ N = 6
 TC = 64
 NO = N * TC
 KC = NO // 16
+NT = N + 1
 FAR = 1024
+ZA = NO
+ZB = NO + 8
+WW = NO + 16
+NCORES = 96
 
 SCRATCH = {
-    "win": ("sbuf", [128, NO + 8], "bfloat16"),
+    "win": ("sbuf", [128, WW], "bfloat16"),
     "zz": ("sbuf", [128, 8], "bfloat16"),
     "yb": ("sbuf", [128, NO], "bfloat16"),
     "xd": ("dram", [128, TC], "bfloat16"),
@@ -25,14 +30,15 @@ SCRATCH = {
     "ones": ("sbuf", [16, 128], "bfloat16"),
     "cst": ("sbuf", [16, 2 * N], "bfloat16"),
     "ps": ("psum", [128, 2 * N], "float32"),
-    "pp": ("sbuf", [128, 8 * KC], "float32"),
-    "q1": ("sbuf", [128, 4 * KC], "float32"),
-    "q2": ("sbuf", [128, 2 * KC], "float32"),
-    "q3": ("sbuf", [128, KC], "float32"),
-    "off": ("sbuf", [128, KC], "uint16"),
+    "jj": ("sbuf", [128, KC], "float32"),
+    "pp": ("sbuf", [128, NT * KC], "float32"),
+    "mk": ("sbuf", [128, NT * KC], "float32"),
+    "sc": ("sbuf", [128, NT * KC], "float32"),
+    "offe": ("sbuf", [128, KC], "uint16"),
+    "offl": ("sbuf", [128, KC], "uint16"),
 }
-SEMAPHORES = ["ldx", "ldl", "gi", "vc", "vj", "vk", "vl", "vr", "mm", "vm", "vt", "ldd", "lda", "pa", "pd", "p1",
-              "p2", "snt", "gat", "st", "vz", "pz"]
+SEMAPHORES = ["ldx", "ldl", "ldd", "gi", "vz", "vo", "vn", "vc", "vj", "vk", "vl", "vr", "mm", "vm", "vs", "ve", "vf",
+              "pz", "pc", "pd", "pe", "pl", "snt", "ge", "gl", "ste", "stl"]
 
 
 def _bits(m):
@@ -45,36 +51,27 @@ def _plan(cores, topo):
         if topo.chip(c) not in chips:
             chips.append(topo.chip(c))
     members = {ch: [c for c in cores if topo.chip(c) == ch] for ch in chips}
-    slot, first, k = {}, {}, 0
+    idle = {}
     for ch in chips:
-        first[ch] = k
-        for c in members[ch]:
-            slot[c] = k
-            k += 1
-    carry = {c: [] for c in cores}
-    for ch in chips:
-        todo = [o for o in chips if o != ch]
-        able = {o: [c for c in members[ch] if all(topo.may_write(c, d) for d in members[o])] for o in todo}
-        todo.sort(key=lambda o: len(able[o]))
+        die = topo.die(members[ch][0])
+        idle[ch] = [c for c in range(NCORES) if topo.chip(c) == ch and c not in cores
+                    and all(topo.may_write(c, d) for d in cores)]
+        idle[ch].sort(key=lambda c: 0 if topo.die(c) == die else 1)
+    direct = {a: [b for b in cores if b != a and topo.may_write(a, b)] for a in cores}
+    relay, lanes, used = [], {a: [] for a in cores}, {ch: [] for ch in chips}
+    for a in cores:
+        ch = topo.chip(a)
+        todo = [o for o in chips if any(not topo.may_write(a, d) for d in members[o])]
+        todo.sort(key=lambda o: 1 if topo.mates(ch, o) else 0)
         for o in todo:
-            carry[min(able[o], key=lambda c: len(carry[c]))].append(o)
-    feed = {c: [d for d in members[topo.chip(c)] if d != c] for c in cores}
-    ahead, relay, lane = [], [], {}
-    for s in cores:
-        ch = topo.chip(s)
-        far = [d for o in carry[s] for d in members[o]]
-        if len(carry[s]) > 1:
-            ahead.append((s, slot[s], far))
-            for f in members[ch]:
-                if f != s:
-                    lane[f] = s
-                    relay.append((s, slot[f], slot[f] + 1, far, True))
-        elif far:
-            relay.append((s, first[ch], first[ch] + len(members[ch]), far, False))
-    return slot, feed, ahead, relay, lane
+            w = [c for c in idle[ch] if c not in used[ch]][0]
+            used[ch].append(w)
+            relay.append((w, a, members[o]))
+            lanes[a].append(w)
+    return members, used, direct, relay, lanes
 
 
-def _mask(core, cores, topo):
+def _off_chip(core, cores, topo):
     m = -1
     for d in cores:
         if d != core:
@@ -83,134 +80,145 @@ def _mask(core, cores, topo):
 
 
 def rank_program(g, core, T, topo):
-    if T.rank_of(core) is None:
+    cores = list(T.cores)
+    members, used, direct, relay, lanes = _plan(cores, topo)
+    here = topo.chip(core)
+    if T.rank_of(core) is None and (here not in used or core not in used[here]):
         return
     S = T.sem
     A = AluOpType
-    cores = list(T.cores)
-    slot, feed, ahead, relay, lane = _plan(cores, topo)
-
-    def engines(c):
-        return _mask(c, cores, topo)
-
-    mask = engines(core)
-    pre = [w for w in ahead if w[0] == core]
-    got = [w for w in ahead if core in w[2]]
-    mine = [w for w in relay if w[0] == core]
-    na = sum(_bits(engines(w[0])) for w in got)
-    nd = sum(_bits(engines(f)) for f in lane if lane[f] == core)
-    n1 = sum(_bits(engines(c)) for c in cores if core in feed[c])
-    n2 = sum(_bits(engines(w[0])) for w in relay if core in w[3])
+    v = g.vector
+    rank = {c: T.rank_of(c) for c in cores}
     sent = [0]
 
-    def send(src, dst, dsts, sem):
+    def moff(c):
+        return _off_chip(c, cores, topo)
+
+    def zb_from(b):
+        u = used[topo.chip(b)]
+        return u[members[topo.chip(b)].index(b) % len(u)]
+
+    def split(b):
+        return TC * (1 + max(rank[a] for (w, a, ds) in relay if b in ds))
+
+    def semname(a, b):
+        return "pe" if rank[a] * TC >= split(b) else "pl"
+
+    def send(sem, src, dst, ds):
         g.remote_dma_fused(
-            [RemoteDMATransfer(dst_ids=[DstId(rid=topo.addr(d)[0], pnc=topo.addr(d)[1]) for d in dsts],
-                               dma_engine_mask=mask, remote_sem=sem, srcs=[src], dsts=[dst for d in dsts])],
+            [RemoteDMATransfer(dst_ids=[DstId(rid=topo.addr(d)[0], pnc=topo.addr(d)[1]) for d in ds],
+                               dma_engine_mask=moff(core), remote_sem=sem, srcs=[src], dsts=[dst for d in ds])],
             local_sem=S.snt)
-        sent[0] += _bits(mask)
+        sent[0] += _bits(moff(core))
 
-    def slots(lo, hi):
-        return T.win[:, lo * TC:hi * TC]
+    def slot(r):
+        return T.win[:, r * TC:(r + 1) * TC]
 
-    k = slot[core]
-    own = slots(k, k + 1)
-    long_rows = core in lane or len(pre) > 0
-    v = g.vector
+    if T.rank_of(core) is None:
+        v.memset(T.zz[:], 0.0).then_inc(S.vz, 1)
+        g.wait_ge(S.vz, 1)
+        send(S.pc, T.zz[:], T.win[:, ZB:ZB + 8], [b for b in members[here] if zb_from(b) == core])
+        g.wait_ge(S.pd, sum(_bits(moff(a)) for a in cores if core in lanes[a]))
+        for (w, a, ds) in relay:
+            if w == core:
+                send(S.pl, T.xr[rank[a]], slot(rank[a]), ds)
+        g.wait_ge(S.snt, sent[0])
+        return
 
-    if long_rows:
-        g.sync.dma_start(T.xd[:], T.x[:]).then_inc(S.ldd, 16)
-    g.sync.dma_start(own, T.x[:]).then_inc(S.ldx, 16)
+    me = rank[core]
+    mates_here = [d for d in members[here] if d != core]
+    SP = split(core)
+    ke = SP // 16
+    nz = sum(_bits(moff(a)) for a in mates_here)
+    nzb = _bits(moff(zb_from(core)))
+    cnt = {"pe": 0, "pl": 0}
+    for a in cores:
+        if core in direct[a]:
+            cnt[semname(a, core)] += _bits(moff(a))
+    for (w, a, ds) in relay:
+        if core in ds:
+            cnt["pl"] += _bits(moff(w))
+
+    g.sync.dma_start(T.xd[:], T.x[:]).then_inc(S.ldd, 16)
+    g.sync.dma_start(slot(me), T.x[:]).then_inc(S.ldx, 16)
     g.scalar.dma_start(T.lnb[:], T.ln[:]).then_inc(S.ldl, 16)
-    if got:
-        g.scalar.wait_ge(S.pa, na)
-        for w in got:
-            g.scalar.dma_start(slots(w[1], w[1] + 1), T.xr[w[1]]).then_inc(S.lda, 16)
 
     v.memset(T.zz[:], 0.0).then_inc(S.vz, 1)
     g.iota(T.vi[:], [[128, KC]], 0, 1).then_inc(S.gi, 1)
     g.wait_ge(S.vz, 1)
-    send(T.zz[:], T.win[:, NO:NO + 8], feed[core], S.pz)
-    if long_rows:
-        g.wait_ge(S.ldd, 16)
-        if core in lane:
-            send(T.xd[:], T.xr[k], [lane[core]], S.pd)
-        for w in pre:
-            send(T.xd[:], T.xr[k], w[2], S.pa)
-        send(T.xd[:], own, feed[core], S.p1)
-    else:
-        g.wait_ge(S.ldx, 16)
-        send(own, own, feed[core], S.p1)
-    if nd:
-        g.wait_ge(S.pd, nd)
-    for w in mine:
-        if w[4]:
-            send(T.xr[w[1]], slots(w[1], w[2]), w[3], S.p2)
-    for w in mine:
-        if not w[4]:
-            g.wait_ge(S.ldx, 16)
-            g.wait_ge(S.p1, n1)
-            send(slots(w[1], w[2]), slots(w[1], w[2]), w[3], S.p2)
+    send(S.pz, T.zz[:], T.win[:, ZA:ZA + 8], mates_here)
+    g.wait_ge(S.ldd, 16)
+    if lanes[core]:
+        send(S.pd, T.xd[:], T.xr[me], lanes[core])
+    groups = {}
+    for b in direct[core]:
+        groups.setdefault(semname(core, b), []).append(b)
+    for sn, ds in groups.items():
+        send(S[sn], T.xd[:], slot(me), ds)
     g.wait_ge(S.snt, sent[0])
 
-    nc = 0
-    v.memset(T.ones[:], 1.0).then_inc(S.vc, 1)
-    v.memset(T.cst[0:1, 0:N], 0.0).then_inc(S.vc, 1)
-    v.memset(T.pp[:, 7 * KC:8 * KC], 0.0).then_inc(S.vc, 1)
-    nc += 3
-    for i in range(N):
-        d = (slot[cores[i + 1]] - slot[cores[i]]) * TC if i + 1 < N else FAR
-        v.memset(T.cst[0:1, N + i:N + i + 1], float(d)).then_inc(S.vc, 1)
-        nc += 1
+    v.memset(T.mk[:], 1.0).then_inc(S.vn, 1)
+    v.memset(T.ones[:], 1.0).then_inc(S.vo, 1)
+    v.memset(T.cst[0:1, 0:N], 0.0).then_inc(S.vo, 1)
+    v.memset(T.cst[0:1, N:2 * N - 1], float(TC)).then_inc(S.vo, 1)
+    v.memset(T.cst[0:1, 2 * N - 1:2 * N], float(FAR)).then_inc(S.vo, 1)
     v.wait_ge(S.gi, 1)
     v.tensor_scalar(T.va[:], T.vi[:], 15, None, A.bitwise_and).then_inc(S.vj, 1)
     v.tensor_scalar(T.vq[:], T.vi[0:16, 0:N], 7, None, A.logical_shift_right).then_inc(S.vj, 1)
     v.tensor_scalar(T.vb[:], T.vi[:], 3, 0xFFF0, A.logical_shift_right, A.bitwise_and).then_inc(S.vj, 1)
+    v.wait_ge(S.vn, 1)
+    v.memset(T.mk[:, 0:NT * KC:NT], 0.0).then_inc(S.vc, 1)
     v.wait_ge(S.vj, 3)
     v.tensor_tensor(T.ki[:], T.vq[:], T.va[0:16, 0:N], A.subtract).then_inc(S.vk, 1)
-    jj = T.pp[:, 6 * KC:7 * KC]
-    v.tensor_tensor(jj, T.va[:], T.vb[:], A.add).then_inc(S.vc, 1)
+    v.tensor_tensor(T.jj[:], T.va[:], T.vb[:], A.add).then_inc(S.vc, 1)
+    v.tensor_tensor(T.pp[:, 0:NT * KC:NT], T.va[:], T.vb[:], A.add).then_inc(S.vc, 1)
     v.wait_ge(S.vk, 1)
     v.tensor_scalar(T.tri[:, 0:N], T.ki[:], 0.0, None, A.is_ge).then_inc(S.vc, 1)
     v.tensor_scalar(T.tri[:, N:2 * N], T.ki[:], 0.0, -1.0, A.is_equal, A.mult).then_inc(S.vc, 1)
-    nc += 3
 
     v.wait_ge(S.ldl, 16)
     v.tensor_copy(T.lnf[:], T.lnb[:, 0:1]).then_inc(S.vl, 1)
     v.wait_ge(S.vl, 1)
-    v.wait_ge(S.vc, nc)
+    v.wait_ge(S.vc, 5)
     v.tensor_scalar(T.rr[:], T.tri[:], T.lnf[:, 0:1], None, A.mult).then_inc(S.vr, 1)
     t = g.tensor
-    t.wait_ge(S.vc, nc)
+    t.wait_ge(S.vo, 4)
     t.matmul(T.ps[:], T.ones[0:1, :], T.cst[0:1, :], True, False)
     t.wait_ge(S.vr, 1)
     t.matmul(T.ps[:], T.ones[:], T.rr[:], False, True).then_inc(S.mm, 1)
     v.wait_ge(S.mm, 1)
     for s in range(N):
-        v.tensor_scalar(T.pp[:, s * KC:(s + 1) * KC], jj, T.ps[:, s:s + 1], T.ps[:, N + s:N + s + 1],
+        v.tensor_scalar(T.pp[:, s + 1:NT * KC:NT], T.jj[:], T.ps[:, s:s + 1], T.ps[:, N + s:N + s + 1],
                         A.is_ge, A.mult).then_inc(S.vm, 1)
     v.wait_ge(S.vm, N)
-    v.tensor_tensor(T.q1[:], T.pp[:, 0:4 * KC], T.pp[:, 4 * KC:8 * KC], A.add).then_inc(S.vt, 1)
-    v.wait_ge(S.vt, 1)
-    v.tensor_tensor(T.q2[:], T.q1[:, 0:2 * KC], T.q1[:, 2 * KC:4 * KC], A.add).then_inc(S.vt, 1)
-    v.wait_ge(S.vt, 2)
-    v.tensor_tensor(T.q3[:], T.q2[:, 0:KC], T.q2[:, KC:2 * KC], A.add).then_inc(S.vt, 1)
-    v.wait_ge(S.vt, 3)
-    v.tensor_scalar(T.off[:], T.q3[:], float(NO), None, A.min).then_inc(S.vt, 1)
+    v.tensor_tensor_scan(T.sc[:], T.mk[:], T.pp[:], 0.0, A.mult, A.add).then_inc(S.vs, 1)
+    v.wait_ge(S.vs, 1)
+    v.tensor_scalar(T.offe[:, ke:KC], T.sc[:, NT * ke + N:NT * KC:NT], float(ZA), float(-SP),
+                    A.min, A.add).then_inc(S.ve, 1)
+    v.tensor_scalar(T.offl[:, 0:ke], T.sc[:, N:NT * ke:NT], float(ZB), None, A.min).then_inc(S.vf, 1)
 
-    window = T.win[:, 0:NO + 8]
-    hk = KC // 2
+    early = T.win[:, SP:ZA + 8]
+    he = (ke + KC) // 2
     for q in (v, g.scalar):
-        q.wait_ge(S.vt, 4)
-        q.wait_ge(S.pz, n1)
+        q.wait_ge(S.ve, 1)
+        q.wait_ge(S.pz, nz)
         q.wait_ge(S.ldx, 16)
-        if got:
-            q.wait_ge(S.lda, 16 * len(got))
-        q.wait_ge(S.p1, n1)
-        q.wait_ge(S.p2, n2)
-    v.tensor_copy(T.yb[:, 0:16 * hk], window.indirect(T.off[:, 0:hk])).then_inc(S.gat, 1)
-    g.scalar.activation(T.yb[:, 16 * hk:NO], window.indirect(T.off[:, hk:KC]),
-                        ActivationFunctionType.Identity, bias=-0.0, scale=1.0).then_inc(S.gat, 1)
-    g.sync.wait_ge(S.gat, 2)
-    g.sync.dma_start(T.y[:], T.yb[:]).then_inc(S.st, 16)
-    g.sync.wait_ge(S.st, 16)
+        q.wait_ge(S.pe, cnt["pe"])
+    v.tensor_copy(T.yb[:, SP:16 * he], early.indirect(T.offe[:, ke:he])).then_inc(S.ge, 1)
+    g.scalar.activation(T.yb[:, 16 * he:NO], early.indirect(T.offe[:, he:KC]),
+                        ActivationFunctionType.Identity, bias=-0.0, scale=1.0).then_inc(S.ge, 1)
+    whole = T.win[:, 0:WW]
+    hl = ke // 2
+    for q in (v, g.scalar):
+        q.wait_ge(S.vf, 1)
+        q.wait_ge(S.pc, nzb)
+        q.wait_ge(S.pl, cnt["pl"])
+    v.tensor_copy(T.yb[:, 0:16 * hl], whole.indirect(T.offl[:, 0:hl])).then_inc(S.gl, 1)
+    g.scalar.activation(T.yb[:, 16 * hl:SP], whole.indirect(T.offl[:, hl:ke]),
+                        ActivationFunctionType.Identity, bias=-0.0, scale=1.0).then_inc(S.gl, 1)
+    g.sync.wait_ge(S.ge, 2)
+    g.sync.dma_start(T.y[:, SP:NO], T.yb[:, SP:NO]).then_inc(S.ste, 16)
+    g.sync.wait_ge(S.gl, 2)
+    g.sync.dma_start(T.y[:, 0:SP], T.yb[:, 0:SP]).then_inc(S.stl, 16)
+    g.sync.wait_ge(S.ste, 16)
+    g.sync.wait_ge(S.stl, 16)

from concourse.bass import DstId, RemoteDMATransfer
from concourse.mybir import AluOpType, ActivationFunctionType

N = 6
TC = 64
NO = N * TC
KC = NO // 16
NT = N + 1
FAR = 1024
ZA = NO
ZB = NO + 8
WW = NO + 16
NCORES = 96

SCRATCH = {
    "win": ("sbuf", [128, WW], "bfloat16"),
    "zz": ("sbuf", [128, 8], "bfloat16"),
    "yb": ("sbuf", [128, NO], "bfloat16"),
    "xd": ("dram", [128, TC], "bfloat16"),
    "xr": ("dram", [N, 128, TC], "bfloat16"),
    "lnb": ("sbuf", [16, 2], "int32"),
    "lnf": ("sbuf", [16, 1], "float32"),
    "vi": ("sbuf", [128, KC], "int32"),
    "va": ("sbuf", [128, KC], "int32"),
    "vb": ("sbuf", [128, KC], "int32"),
    "vq": ("sbuf", [16, N], "int32"),
    "ki": ("sbuf", [16, N], "float32"),
    "tri": ("sbuf", [16, 2 * N], "bfloat16"),
    "rr": ("sbuf", [16, 2 * N], "bfloat16"),
    "ones": ("sbuf", [16, 128], "bfloat16"),
    "cst": ("sbuf", [16, 2 * N], "bfloat16"),
    "ps": ("psum", [128, 2 * N], "float32"),
    "jj": ("sbuf", [128, KC], "float32"),
    "pp": ("sbuf", [128, NT * KC], "float32"),
    "mk": ("sbuf", [128, NT * KC], "float32"),
    "sc": ("sbuf", [128, NT * KC], "float32"),
    "offe": ("sbuf", [128, KC], "uint16"),
    "offl": ("sbuf", [128, KC], "uint16"),
}
SEMAPHORES = ["ldx", "ldl", "ldd", "gi", "vz", "vo", "vn", "vc", "vj", "vk", "vl", "vr", "mm", "vm", "vs", "ve", "vf",
              "pz", "pc", "pd", "pe", "pl", "snt", "ge", "gl", "ste", "stl"]


def _bits(m):
    return bin(m).count("1")


def _plan(cores, topo):
    chips = []
    for c in cores:
        if topo.chip(c) not in chips:
            chips.append(topo.chip(c))
    members = {ch: [c for c in cores if topo.chip(c) == ch] for ch in chips}
    idle = {}
    for ch in chips:
        die = topo.die(members[ch][0])
        idle[ch] = [c for c in range(NCORES) if topo.chip(c) == ch and c not in cores
                    and all(topo.may_write(c, d) for d in cores)]
        idle[ch].sort(key=lambda c: 0 if topo.die(c) == die else 1)
    direct = {a: [b for b in cores if b != a and topo.may_write(a, b)] for a in cores}
    relay, lanes, used = [], {a: [] for a in cores}, {ch: [] for ch in chips}
    for a in cores:
        ch = topo.chip(a)
        todo = [o for o in chips if any(not topo.may_write(a, d) for d in members[o])]
        todo.sort(key=lambda o: 1 if topo.mates(ch, o) else 0)
        for o in todo:
            w = [c for c in idle[ch] if c not in used[ch]][0]
            used[ch].append(w)
            relay.append((w, a, members[o]))
            lanes[a].append(w)
    return members, used, direct, relay, lanes


def _off_chip(core, cores, topo):
    m = -1
    for d in cores:
        if d != core:
            m &= topo.mask(core, d)
    return m


def rank_program(g, core, T, topo):
    cores = list(T.cores)
    members, used, direct, relay, lanes = _plan(cores, topo)
    here = topo.chip(core)
    if T.rank_of(core) is None and (here not in used or core not in used[here]):
        return
    S = T.sem
    A = AluOpType
    v = g.vector
    rank = {c: T.rank_of(c) for c in cores}
    sent = [0]

    def moff(c):
        return _off_chip(c, cores, topo)

    def zb_from(b):
        u = used[topo.chip(b)]
        return u[members[topo.chip(b)].index(b) % len(u)]

    def split(b):
        return TC * (1 + max(rank[a] for (w, a, ds) in relay if b in ds))

    def semname(a, b):
        return "pe" if rank[a] * TC >= split(b) else "pl"

    def send(sem, src, dst, ds):
        g.remote_dma_fused(
            [RemoteDMATransfer(dst_ids=[DstId(rid=topo.addr(d)[0], pnc=topo.addr(d)[1]) for d in ds],
                               dma_engine_mask=moff(core), remote_sem=sem, srcs=[src], dsts=[dst for d in ds])],
            local_sem=S.snt)
        sent[0] += _bits(moff(core))

    def slot(r):
        return T.win[:, r * TC:(r + 1) * TC]

    if T.rank_of(core) is None:
        v.memset(T.zz[:], 0.0).then_inc(S.vz, 1)
        g.wait_ge(S.vz, 1)
        send(S.pc, T.zz[:], T.win[:, ZB:ZB + 8], [b for b in members[here] if zb_from(b) == core])
        g.wait_ge(S.pd, sum(_bits(moff(a)) for a in cores if core in lanes[a]))
        for (w, a, ds) in relay:
            if w == core:
                send(S.pl, T.xr[rank[a]], slot(rank[a]), ds)
        g.wait_ge(S.snt, sent[0])
        return

    me = rank[core]
    mates_here = [d for d in members[here] if d != core]
    SP = split(core)
    ke = SP // 16
    nz = sum(_bits(moff(a)) for a in mates_here)
    nzb = _bits(moff(zb_from(core)))
    cnt = {"pe": 0, "pl": 0}
    for a in cores:
        if core in direct[a]:
            cnt[semname(a, core)] += _bits(moff(a))
    for (w, a, ds) in relay:
        if core in ds:
            cnt["pl"] += _bits(moff(w))

    g.sync.dma_start(T.xd[:], T.x[:]).then_inc(S.ldd, 16)
    g.sync.dma_start(slot(me), T.x[:]).then_inc(S.ldx, 16)
    g.scalar.dma_start(T.lnb[:], T.ln[:]).then_inc(S.ldl, 16)

    v.memset(T.zz[:], 0.0).then_inc(S.vz, 1)
    g.iota(T.vi[:], [[128, KC]], 0, 1).then_inc(S.gi, 1)
    g.wait_ge(S.vz, 1)
    send(S.pz, T.zz[:], T.win[:, ZA:ZA + 8], mates_here)
    g.wait_ge(S.ldd, 16)
    if lanes[core]:
        send(S.pd, T.xd[:], T.xr[me], lanes[core])
    groups = {}
    for b in direct[core]:
        groups.setdefault(semname(core, b), []).append(b)
    for sn, ds in groups.items():
        send(S[sn], T.xd[:], slot(me), ds)
    g.wait_ge(S.snt, sent[0])

    v.memset(T.mk[:], 1.0).then_inc(S.vn, 1)
    v.memset(T.ones[:], 1.0).then_inc(S.vo, 1)
    v.memset(T.cst[0:1, 0:N], 0.0).then_inc(S.vo, 1)
    v.memset(T.cst[0:1, N:2 * N - 1], float(TC)).then_inc(S.vo, 1)
    v.memset(T.cst[0:1, 2 * N - 1:2 * N], float(FAR)).then_inc(S.vo, 1)
    v.wait_ge(S.gi, 1)
    v.tensor_scalar(T.va[:], T.vi[:], 15, None, A.bitwise_and).then_inc(S.vj, 1)
    v.tensor_scalar(T.vq[:], T.vi[0:16, 0:N], 7, None, A.logical_shift_right).then_inc(S.vj, 1)
    v.tensor_scalar(T.vb[:], T.vi[:], 3, 0xFFF0, A.logical_shift_right, A.bitwise_and).then_inc(S.vj, 1)
    v.wait_ge(S.vn, 1)
    v.memset(T.mk[:, 0:NT * KC:NT], 0.0).then_inc(S.vc, 1)
    v.wait_ge(S.vj, 3)
    v.tensor_tensor(T.ki[:], T.vq[:], T.va[0:16, 0:N], A.subtract).then_inc(S.vk, 1)
    v.tensor_tensor(T.jj[:], T.va[:], T.vb[:], A.add).then_inc(S.vc, 1)
    v.tensor_tensor(T.pp[:, 0:NT * KC:NT], T.va[:], T.vb[:], A.add).then_inc(S.vc, 1)
    v.wait_ge(S.vk, 1)
    v.tensor_scalar(T.tri[:, 0:N], T.ki[:], 0.0, None, A.is_ge).then_inc(S.vc, 1)
    v.tensor_scalar(T.tri[:, N:2 * N], T.ki[:], 0.0, -1.0, A.is_equal, A.mult).then_inc(S.vc, 1)

    v.wait_ge(S.ldl, 16)
    v.tensor_copy(T.lnf[:], T.lnb[:, 0:1]).then_inc(S.vl, 1)
    v.wait_ge(S.vl, 1)
    v.wait_ge(S.vc, 5)
    v.tensor_scalar(T.rr[:], T.tri[:], T.lnf[:, 0:1], None, A.mult).then_inc(S.vr, 1)
    t = g.tensor
    t.wait_ge(S.vo, 4)
    t.matmul(T.ps[:], T.ones[0:1, :], T.cst[0:1, :], True, False)
    t.wait_ge(S.vr, 1)
    t.matmul(T.ps[:], T.ones[:], T.rr[:], False, True).then_inc(S.mm, 1)
    v.wait_ge(S.mm, 1)
    for s in range(N):
        v.tensor_scalar(T.pp[:, s + 1:NT * KC:NT], T.jj[:], T.ps[:, s:s + 1], T.ps[:, N + s:N + s + 1],
                        A.is_ge, A.mult).then_inc(S.vm, 1)
    v.wait_ge(S.vm, N)
    v.tensor_tensor_scan(T.sc[:], T.mk[:], T.pp[:], 0.0, A.mult, A.add).then_inc(S.vs, 1)
    v.wait_ge(S.vs, 1)
    v.tensor_scalar(T.offe[:, ke:KC], T.sc[:, NT * ke + N:NT * KC:NT], float(ZA), float(-SP),
                    A.min, A.add).then_inc(S.ve, 1)
    v.tensor_scalar(T.offl[:, 0:ke], T.sc[:, N:NT * ke:NT], float(ZB), None, A.min).then_inc(S.vf, 1)

    early = T.win[:, SP:ZA + 8]
    he = (ke + KC) // 2
    for q in (v, g.scalar):
        q.wait_ge(S.ve, 1)
        q.wait_ge(S.pz, nz)
        q.wait_ge(S.ldx, 16)
        q.wait_ge(S.pe, cnt["pe"])
    v.tensor_copy(T.yb[:, SP:16 * he], early.indirect(T.offe[:, ke:he])).then_inc(S.ge, 1)
    g.scalar.activation(T.yb[:, 16 * he:NO], early.indirect(T.offe[:, he:KC]),
                        ActivationFunctionType.Identity, bias=-0.0, scale=1.0).then_inc(S.ge, 1)
    whole = T.win[:, 0:WW]
    hl = ke // 2
    for q in (v, g.scalar):
        q.wait_ge(S.vf, 1)
        q.wait_ge(S.pc, nzb)
        q.wait_ge(S.pl, cnt["pl"])
    v.tensor_copy(T.yb[:, 0:16 * hl], whole.indirect(T.offl[:, 0:hl])).then_inc(S.gl, 1)
    g.scalar.activation(T.yb[:, 16 * hl:SP], whole.indirect(T.offl[:, hl:ke]),
                        ActivationFunctionType.Identity, bias=-0.0, scale=1.0).then_inc(S.gl, 1)
    g.sync.wait_ge(S.ge, 2)
    g.sync.dma_start(T.y[:, SP:NO], T.yb[:, SP:NO]).then_inc(S.ste, 16)
    g.sync.wait_ge(S.gl, 2)
    g.sync.dma_start(T.y[:, 0:SP], T.yb[:, 0:SP]).then_inc(S.stl, 16)
    g.sync.wait_ge(S.ste, 16)
    g.sync.wait_ge(S.stl, 16)
